import numpy as np
import ml_dtypes


def mxq(x, axis, fmt="e4m3"):
    dtype, down = {"e4m3": (ml_dtypes.float8_e4m3fn, 7), "e5m2": (ml_dtypes.float8_e5m2, 14)}[fmt]
    v = np.moveaxis(np.asarray(x, np.float32).astype(ml_dtypes.bfloat16).astype(np.float64), axis, -1)
    blocks = v.reshape(v.shape[:-1] + (-1, 32))
    amax = np.abs(blocks).max(-1, keepdims=True)
    byte = np.maximum(np.where(amax > 0, np.frexp(amax)[1] - 1 + 127, 0) - down, 1)
    scale = np.exp2(byte - 127.0)
    codes = (blocks / scale).astype(np.float32).astype(dtype).astype(np.float64)
    return np.moveaxis((codes * scale).reshape(v.shape), -1, axis)


WIDE = False


def mx_kscale(k):
    if not WIDE:
        return np.ones(k)
    levels = np.array([30, -30])
    if k % 512:
        return np.exp2(np.random.permutation(np.resize(levels, k // 32))).repeat(32)
    a = np.empty((k // 512, 16))
    for p in range(k // 512):
        a[p, :8] = np.random.permutation(np.resize(levels, 8))
        for g in range(8):
            far = levels[np.abs(levels - a[p, g]) >= 10]
            a[p, g + 8] = far[np.random.randint(len(far))]
    return np.exp2(a.ravel()).repeat(32)


def f64(x):
    return np.asarray(x).astype(np.float64)


def striped(idx):
    return np.tile(np.asarray(idx).reshape(-1, 16).T, (8, 1)).astype(np.uint16)


def unstriped(offs):
    return offs[:16].T.reshape(-1).astype(np.int64)


E2M1 = np.array([0.0, 0.5, 1.0, 1.5, 2.0, 3.0, 4.0, 6.0, -0.0, -0.5, -1.0, -1.5, -2.0, -3.0, -4.0, -6.0])


def pack_weight(w, fmt):
    k, n = w.shape
    w = f64(np.asarray(w, np.float32).astype(ml_dtypes.bfloat16)).reshape(k // 32, 32, n)
    amax = np.abs(w).max(1)
    if fmt in ("e4m3", "e5m2"):
        byte = np.frexp(amax)[1] - 1 + 127 - (7 if fmt == "e4m3" else 14)
    else:
        mant, ex = np.frexp(amax / 6.0)
        byte = np.where(mant > 0.5, ex, ex - 1) + 127
    byte = np.clip(np.where(amax > 0, byte, 1), 1, 254)
    scaled = (w * np.exp2(127.0 - byte)[:, None, :]).reshape(k, n).astype(np.float32)
    by_word = np.ascontiguousarray(scaled.reshape(k // 512, 128, 4, n).transpose(0, 1, 3, 2))
    if fmt in ("e4m3", "e5m2"):
        words = by_word.astype(ml_dtypes.float8_e4m3fn if fmt == "e4m3" else ml_dtypes.float8_e5m2).view(np.uint8)
    else:
        c = by_word.astype(ml_dtypes.float4_e2m1fn).view(np.uint8) & 0xF
        words = (c[..., 0::2] | (c[..., 1::2] << 4)).reshape(k // 512, 128, 2 * n)
    return np.ascontiguousarray(words), np.ascontiguousarray(byte.astype(np.uint8).reshape(k // 512, 16, n))


def unpack_weight(words, scales, fmt):
    g, _, n = scales.shape
    words = np.ascontiguousarray(words).reshape(g, 128, n, -1)
    if fmt in ("e4m3", "e5m2"):
        vals = words.view(ml_dtypes.float8_e4m3fn if fmt == "e4m3" else ml_dtypes.float8_e5m2).astype(np.float64)
    else:
        nib = np.empty((g, 128, n, 4), np.uint8)
        nib[..., 0::2] = words & 0xF
        nib[..., 1::2] = words >> 4
        vals = E2M1[nib]
    vals = vals * np.repeat(np.exp2(scales.astype(np.float64) - 127.0), 8, axis=1)[..., None]
    return vals.transpose(0, 1, 3, 2).reshape(g * 512, n)


K, T, J, I, S, C = 1024, 1024, 256, 256, 512, 512


def setup_inputs():
    n = np.random.standard_normal
    idx = np.random.permutation(T)[:J]
    idx2 = np.random.permutation(S)[:J]
    idx3 = np.random.permutation(C)[:I]
    fk = mx_kscale(K)
    kyp = pack_weight(n((K, I)) / fk[:, None], "e5m2")
    return {
        "xf": (n((K, T)) * 0.03).astype(np.float32),
        "xb": (n((K, S))).astype(np.float32),
        "fk": (np.random.uniform(0.5, 2.0, (K, 1)) * fk[:, None]).astype(np.float32),
        "ky_words": kyp[0],
        "ky_scales": kyp[1],
        "bi": (np.random.uniform(-0.7, 0.7, (1, I))).astype(np.float32),
        "tb": (1.0 * n((J, C))).astype(np.float32),
        "offs": striped(idx),
        "offs2": striped(idx2),
        "offs3": striped(idx3),
    }


def reference(xf, xb, fk, ky_words, ky_scales, bi, tb, offs, offs2, offs3):
    idx = unstriped(offs)
    idx2 = unstriped(offs2)
    idx3 = unstriped(offs3)
    kyu = unpack_weight(ky_words, ky_scales, "e5m2")
    u = f64(xf)[:, idx] * f64(xb)[:, idx2] * f64(fk)
    uq = mxq(u, 0, "e5m2")
    a0 = uq.T @ kyu
    a = a0 + f64(bi)
    y = np.tanh(a) * f64(tb)[:, idx3]
    return y

@@ -1,0 +1,140 @@
+from contextlib import ExitStack
+
+import concourse.mybir as mybir
+from concourse.masks import make_identity
+
+K, T, J, I, S, C = 1024, 1024, 256, 256, 512, 512
+FLOPS = 2 * K * J * I
+
+F32 = mybir.dt.float32
+BF16 = mybir.dt.bfloat16
+I32 = mybir.dt.int32
+U32 = mybir.dt.uint32
+U16 = mybir.dt.uint16
+U8 = mybir.dt.uint8
+E5M2X4 = mybir.dt.float8_e5m2_x4
+MULT = mybir.AluOpType.mult
+ADD = mybir.AluOpType.add
+COPY = mybir.ActivationFunctionType.Copy
+TANH = mybir.ActivationFunctionType.Tanh
+
+P = 128
+PACK = 4
+PASSES = K // (P * PACK)
+HALVES = J // P
+LIST_COLS = J // 16
+HALF_COLS = P // 16
+XB_PLANES = 2
+
+
+def tile_list_scores_products_given_tabled_kernel(tc, xf, xb, fk, ky_words, ky_scales, bi, tb, offs, offs2, offs3, out):
+    nc = tc.nc
+    with ExitStack() as ctx:
+        sb = ctx.enter_context(tc.tile_pool(name="sb", bufs=1))
+        ps = ctx.enter_context(tc.psum_pool(name="ps", bufs=1))
+
+        xf_planes = xf.rearrange("(z p t) n -> z t p n", p=P, t=PACK)
+        xb_pairs = xb.rearrange("(z p g e) s -> z g p e s", p=P, g=PACK // XB_PLANES, e=XB_PLANES)
+
+        list_xf = sb.tile([P, LIST_COLS], U16, name="list_xf")
+        list_xb = sb.tile([P, LIST_COLS], U16, name="list_xb")
+        list_tb = sb.tile([P, LIST_COLS], U16, name="list_tb")
+        fk_sb = sb.tile([P, PASSES, PACK], F32, name="fk_sb")
+        bi_cols = sb.tile([P, HALVES], F32, name="bi_cols")
+        ky_codes = sb.tile([P, PASSES, I], U32, name="ky_codes", align_bytes=64)
+        ky_plane = sb.tile([P, PASSES, I], U8, name="ky_plane", align_bytes=64)
+        xf_sb = {(z, t): sb.tile([P, T], F32, name=f"xf_{z}_{t}") for z in range(PASSES) for t in range(PACK)}
+        xb_sb = {(z, g): sb.tile([P, XB_PLANES, S], F32, name=f"xb_{z}_{g}") for z in range(PASSES) for g in range(PACK // XB_PLANES)}
+        tb_sb = [sb.tile([P, C], F32, name=f"tb_{h}") for h in range(HALVES)]
+
+        nc.gpsimd.memset(ky_plane[:].bitcast(I32), 0)
+        ident = sb.tile([P, P], F32, name="ident")
+        make_identity(nc, ident[:])
+
+        def load_xf(z, t):
+            nc.sync.dma_start(out=xf_sb[z, t][:], in_=xf_planes[z, t])
+
+        def load_xb(z, g):
+            nc.sync.dma_start(out=xb_sb[z, g][:], in_=xb_pairs[z, g])
+
+        def load_scales(q):
+            nc.sync.dma_start(
+                out=ky_plane[32 * q : 32 * q + 4].bitcast(I32),
+                in_=ky_scales[:, 4 * q : 4 * q + 4, :].rearrange("z r c -> r z c").bitcast(I32),
+            )
+
+        load_xb(0, 0)
+        load_xf(0, 0)
+        nc.sync.dma_start(list_xb[:], offs2)
+        nc.sync.dma_start(out=fk_sb[:], in_=fk.rearrange("(z p t) o -> p z (t o)", p=P, t=PACK))
+        nc.sync.dma_start(list_xf[:], offs)
+        load_xf(0, 1)
+        load_xb(0, 1)
+        nc.sync.dma_start(out=bi_cols[:], in_=bi.rearrange("o (p h) -> p (o h)", h=HALVES))
+        load_xf(0, 2)
+        nc.sync.dma_start(list_tb[:], offs3)
+        load_xf(0, 3)
+        load_scales(0)
+        load_xb(1, 0)
+        load_scales(1)
+        load_xf(1, 0)
+        load_scales(2)
+        load_xb(1, 1)
+        load_scales(3)
+        load_xf(1, 1)
+        load_xf(1, 2)
+        load_xf(1, 3)
+        nc.sync.dma_start(out=ky_codes[:].bitcast(I32), in_=ky_words.rearrange("z p c r -> p z (c r)").bitcast(I32))
+        for h in range(HALVES):
+            nc.sync.dma_start(out=tb_sb[h][:], in_=tb[h * P : (h + 1) * P, :])
+
+        acc = [ps.tile([P, I], F32, name=f"acc_{h}") for h in range(HALVES)]
+        for z in range(PASSES):
+            u32 = [sb.tile([P, PACK, P], F32, name=f"u32_{z}_{h}") for h in range(HALVES)]
+            for t in range(PACK):
+                picked = sb.tile([P, J], F32, name=f"picked_{z}_{t}")
+                nc.scalar.activation(picked[:], xb_sb[z, t // XB_PLANES][:, t % XB_PLANES, :].indirect(list_xb[:]), COPY)
+                scaled = sb.tile([P, J], F32, name=f"scaled_{z}_{t}")
+                nc.scalar.activation(scaled[:], picked[:], COPY, scale=fk_sb[:, z, t : t + 1])
+                for h in range(HALVES):
+                    nc.vector.tensor_tensor(
+                        u32[h][:, t, :],
+                        xf_sb[z, t][:].indirect(list_xf[:, h * HALF_COLS : (h + 1) * HALF_COLS]),
+                        scaled[:, h * P : (h + 1) * P],
+                        MULT,
+                    )
+            u16 = [sb.tile([P, P, PACK], BF16, name=f"u16_{z}_{h}", align_bytes=64) for h in range(HALVES)]
+            nc.scalar.copy(out=u16[0][:], in_=u32[0][:].rearrange("p t j -> p j t"))
+            nc.vector.tensor_copy(out=u16[1][:], in_=u32[1][:].rearrange("p t j -> p j t"))
+            for h in range(HALVES):
+                codes = sb.tile([P, P], U32, name=f"codes_{z}_{h}", align_bytes=64)
+                plane = sb.tile([P, P], U8, name=f"plane_{z}_{h}", align_bytes=64)
+                nc.vector.quantize_mx(out=codes[:].bitcast(E5M2X4), scales=plane[:], in_=u16[h][:].rearrange("p j t -> p (j t)"))
+                nc.tensor.matmul_mx(
+                    out=acc[h][:],
+                    lhsT=codes[:].bitcast(E5M2X4),
+                    lhsT_scale=plane[:],
+                    rhs=ky_codes[:, z, :].bitcast(E5M2X4),
+                    rhs_scale=ky_plane[:, z, :],
+                    start=(z == 0),
+                    stop=(z == PASSES - 1),
+                )
+
+        bias_ps = ps.tile([P, HALVES, P], F32, name="bias_ps")
+        for e in range(HALVES):
+            nc.tensor.transpose(bias_ps[:, e, :], bi_cols[:, e : e + 1].to_broadcast([P, P]), ident[:])
+        bias = sb.tile([P, I], F32, name="bias")
+        nc.vector.tensor_copy(out=bias[:].rearrange("p (n e) -> p n e", e=HALVES), in_=bias_ps[:].rearrange("p e n -> p n e"))
+
+        factor = [sb.tile([P, I], F32, name=f"factor_{h}") for h in range(HALVES)]
+        score = [sb.tile([P, I], F32, name=f"score_{h}") for h in range(HALVES)]
+        squashed = [sb.tile([P, I], F32, name=f"squashed_{h}") for h in range(HALVES)]
+        result = [sb.tile([P, I], F32, name=f"result_{h}") for h in range(HALVES)]
+        for h in range(HALVES):
+            nc.scalar.activation(factor[h][:], tb_sb[h][:].indirect(list_tb[:]), COPY)
+        for h in range(HALVES):
+            nc.vector.tensor_tensor(score[h][:], acc[h][:], bias[:], ADD)
+            nc.scalar.activation(squashed[h][:], score[h][:], TANH)
+        for h in range(HALVES):
+            nc.vector.tensor_tensor(result[h][:], squashed[h][:], factor[h][:], MULT)
+            nc.sync.dma_start(out=out[h * P : (h + 1) * P, :], in_=result[h][:])

@@ -24,7 +24,7 @@ PASSES = K // (P * PACK)
 HALVES = J // P
 LIST_COLS = J // 16
 HALF_COLS = P // 16
-XB_PLANES = 2
+XF_LOADS = ((0, 0, 2), (0, 2, 4), (1, 0, 1), (1, 1, 2), (1, 2, 3), (1, 3, 4))
 
 
 def tile_list_scores_products_given_tabled_kernel(tc, xf, xb, fk, ky_words, ky_scales, bi, tb, offs, offs2, offs3, out):
@@ -33,8 +33,8 @@ def tile_list_scores_products_given_tabled_kernel(tc, xf, xb, fk, ky_words, ky_s
         sb = ctx.enter_context(tc.tile_pool(name="sb", bufs=1))
         ps = ctx.enter_context(tc.psum_pool(name="ps", bufs=1))
 
-        xf_planes = xf.rearrange("(z p t) n -> z t p n", p=P, t=PACK)
-        xb_pairs = xb.rearrange("(z p g e) s -> z g p e s", p=P, g=PACK // XB_PLANES, e=XB_PLANES)
+        xf_rows = xf.rearrange("(z p t) n -> z p t n", p=P, t=PACK)
+        xb_rows = xb.rearrange("(z p t) s -> z p t s", p=P, t=PACK)
 
         list_xf = sb.tile([P, LIST_COLS], U16, name="list_xf")
         list_xb = sb.tile([P, LIST_COLS], U16, name="list_xb")
@@ -43,19 +43,20 @@ def tile_list_scores_products_given_tabled_kernel(tc, xf, xb, fk, ky_words, ky_s
         bi_cols = sb.tile([P, HALVES], F32, name="bi_cols")
         ky_codes = sb.tile([P, PASSES, I], U32, name="ky_codes", align_bytes=64)
         ky_plane = sb.tile([P, PASSES, I], U8, name="ky_plane", align_bytes=64)
-        xf_sb = {(z, t): sb.tile([P, T], F32, name=f"xf_{z}_{t}") for z in range(PASSES) for t in range(PACK)}
-        xb_sb = {(z, g): sb.tile([P, XB_PLANES, S], F32, name=f"xb_{z}_{g}") for z in range(PASSES) for g in range(PACK // XB_PLANES)}
-        tb_sb = [sb.tile([P, C], F32, name=f"tb_{h}") for h in range(HALVES)]
+        xf_sb = {(z, t0): sb.tile([P, (t1 - t0) * T], F32, name=f"xf_{z}_{t0}") for z, t0, t1 in XF_LOADS}
+        xb_sb = [sb.tile([P, PACK * S], F32, name=f"xb_{z}") for z in range(PASSES)]
+        tb_sb = [sb.tile([P, C], F32, name=f"tb_{h}", tag=f"tb_{h}") for h in range(HALVES)]
 
         nc.gpsimd.memset(ky_plane[:].bitcast(I32), 0)
         ident = sb.tile([P, P], F32, name="ident")
         make_identity(nc, ident[:])
 
-        def load_xf(z, t):
-            nc.sync.dma_start(out=xf_sb[z, t][:], in_=xf_planes[z, t])
+        def load_xf(n):
+            z, t0, t1 = XF_LOADS[n]
+            nc.sync.dma_start(out=xf_sb[z, t0][:], in_=xf_rows[z, :, t0:t1, :].rearrange("p t n -> p (t n)"))
 
-        def load_xb(z, g):
-            nc.sync.dma_start(out=xb_sb[z, g][:], in_=xb_pairs[z, g])
+        def load_xb(z):
+            nc.sync.dma_start(out=xb_sb[z][:], in_=xb_rows[z].rearrange("p t s -> p (t s)"))
 
         def load_scales(q):
             nc.sync.dma_start(
@@ -63,62 +64,78 @@ def tile_list_scores_products_given_tabled_kernel(tc, xf, xb, fk, ky_words, ky_s
                 in_=ky_scales[:, 4 * q : 4 * q + 4, :].rearrange("z r c -> r z c").bitcast(I32),
             )
 
-        load_xb(0, 0)
-        load_xf(0, 0)
+        load_xb(0)
         nc.sync.dma_start(list_xb[:], offs2)
-        nc.sync.dma_start(out=fk_sb[:], in_=fk.rearrange("(z p t) o -> p z (t o)", p=P, t=PACK))
         nc.sync.dma_start(list_xf[:], offs)
-        load_xf(0, 1)
-        load_xb(0, 1)
+        nc.sync.dma_start(out=fk_sb[:], in_=fk.rearrange("(z p t) o -> p z (t o)", p=P, t=PACK))
         nc.sync.dma_start(out=bi_cols[:], in_=bi.rearrange("o (p h) -> p (o h)", h=HALVES))
-        load_xf(0, 2)
+        load_xf(0)
         nc.sync.dma_start(list_tb[:], offs3)
-        load_xf(0, 3)
-        load_scales(0)
-        load_xb(1, 0)
-        load_scales(1)
-        load_xf(1, 0)
-        load_scales(2)
-        load_xb(1, 1)
-        load_scales(3)
-        load_xf(1, 1)
-        load_xf(1, 2)
-        load_xf(1, 3)
+        load_xf(1)
+        load_xb(1)
+        for n in range(2, len(XF_LOADS)):
+            load_xf(n)
+        for q in range(4):
+            load_scales(q)
         nc.sync.dma_start(out=ky_codes[:].bitcast(I32), in_=ky_words.rearrange("z p c r -> p z (c r)").bitcast(I32))
         for h in range(HALVES):
             nc.sync.dma_start(out=tb_sb[h][:], in_=tb[h * P : (h + 1) * P, :])
 
-        acc = [ps.tile([P, I], F32, name=f"acc_{h}") for h in range(HALVES)]
+        acc = {(h, c): ps.tile([P, P], F32, name=f"acc_{h}_{c}") for h in range(HALVES) for c in range(HALVES)}
+        u32_all = [sb.tile([P, HALVES, PACK, P], F32, name=f"u32_{z}") for z in range(PASSES)]
         for z in range(PASSES):
-            u32 = [sb.tile([P, PACK, P], F32, name=f"u32_{z}_{h}") for h in range(HALVES)]
-            for t in range(PACK):
-                picked = sb.tile([P, J], F32, name=f"picked_{z}_{t}")
-                nc.scalar.activation(picked[:], xb_sb[z, t // XB_PLANES][:, t % XB_PLANES, :].indirect(list_xb[:]), COPY)
-                scaled = sb.tile([P, J], F32, name=f"scaled_{z}_{t}")
-                nc.scalar.activation(scaled[:], picked[:], COPY, scale=fk_sb[:, z, t : t + 1])
-                for h in range(HALVES):
-                    nc.vector.tensor_tensor(
-                        u32[h][:, t, :],
-                        xf_sb[z, t][:].indirect(list_xf[:, h * HALF_COLS : (h + 1) * HALF_COLS]),
-                        scaled[:, h * P : (h + 1) * P],
-                        MULT,
-                    )
-            u16 = [sb.tile([P, P, PACK], BF16, name=f"u16_{z}_{h}", align_bytes=64) for h in range(HALVES)]
-            nc.scalar.copy(out=u16[0][:], in_=u32[0][:].rearrange("p t j -> p j t"))
-            nc.vector.tensor_copy(out=u16[1][:], in_=u32[1][:].rearrange("p t j -> p j t"))
+            u32 = u32_all[z]
+            picked_xb = [sb.tile([P, J], F32, name=f"picked_xb_{z}_{t}") for t in range(PACK)]
+            if z == 0:
+                for t in range(PACK):
+                    window = xb_sb[z][:, t * S : (t + 1) * S].indirect(list_xb[:])
+                    if t < 2:
+                        nc.vector.tensor_copy(picked_xb[t][:], window)
+                    else:
+                        nc.scalar.activation(picked_xb[t][:], window, COPY)
+                for t0 in (0, 2):
+                    picked_xf = [sb.tile([P, J], F32, name=f"picked_xf_{t}") for t in (t0, t0 + 1)]
+                    nc.vector.tensor_copy(picked_xf[0][:], xf_sb[z, t0][:, 0:T].indirect(list_xf[:]))
+                    nc.scalar.activation(picked_xf[1][:], xf_sb[z, t0][:, T : 2 * T].indirect(list_xf[:]), COPY)
+                    for t in (t0, t0 + 1):
+                        nc.vector.scalar_tensor_tensor(
+                            out=u32[:, :, t, :],
+                            in0=picked_xf[t - t0][:].rearrange("p (h j) -> p h j", h=HALVES),
+                            scalar=fk_sb[:, z, t : t + 1],
+                            in1=picked_xb[t][:].rearrange("p (h j) -> p h j", h=HALVES),
+                            op0=MULT,
+                            op1=MULT,
+                        )
+            else:
+                for t in range(PACK):
+                    nc.scalar.activation(picked_xb[t][:], xb_sb[z][:, t * S : (t + 1) * S].indirect(list_xb[:]), COPY)
+                    scaled = sb.tile([P, J], F32, name=f"scaled_{t}")
+                    nc.scalar.activation(scaled[:], picked_xb[t][:], COPY, scale=fk_sb[:, z, t : t + 1])
+                    for h in range(HALVES):
+                        nc.vector.tensor_tensor(
+                            u32[:, h, t, :],
+                            xf_sb[z, t][:].indirect(list_xf[:, h * HALF_COLS : (h + 1) * HALF_COLS]),
+                            scaled[:, h * P : (h + 1) * P],
+                            MULT,
+                        )
+            u16 = [sb.tile([P, P, PACK], BF16, name=f"u16_{z}_{h}", tag=f"u16_{z}_{h}", align_bytes=64) for h in range(HALVES)]
+            for t0, t1 in ((0, PACK),) if z == 0 else ((0, 2), (2, PACK)):
+                nc.scalar.copy(out=u16[0][:, :, t0:t1], in_=u32[:, 0, t0:t1, :].rearrange("p t j -> p j t"))
+                nc.vector.tensor_copy(out=u16[1][:, :, t0:t1], in_=u32[:, 1, t0:t1, :].rearrange("p t j -> p j t"))
             for h in range(HALVES):
                 codes = sb.tile([P, P], U32, name=f"codes_{z}_{h}", align_bytes=64)
                 plane = sb.tile([P, P], U8, name=f"plane_{z}_{h}", align_bytes=64)
                 nc.vector.quantize_mx(out=codes[:].bitcast(E5M2X4), scales=plane[:], in_=u16[h][:].rearrange("p j t -> p (j t)"))
-                nc.tensor.matmul_mx(
-                    out=acc[h][:],
-                    lhsT=codes[:].bitcast(E5M2X4),
-                    lhsT_scale=plane[:],
-                    rhs=ky_codes[:, z, :].bitcast(E5M2X4),
-                    rhs_scale=ky_plane[:, z, :],
-                    start=(z == 0),
-                    stop=(z == PASSES - 1),
-                )
+                for c in range(HALVES):
+                    nc.tensor.matmul_mx(
+                        out=acc[h, c][:],
+                        lhsT=codes[:].bitcast(E5M2X4),
+                        lhsT_scale=plane[:],
+                        rhs=ky_codes[:, z, c * P : (c + 1) * P].bitcast(E5M2X4),
+                        rhs_scale=ky_plane[:, z, c * P : (c + 1) * P],
+                        start=(z == 0),
+                        stop=(z == PASSES - 1),
+                    )
 
         bias_ps = ps.tile([P, HALVES, P], F32, name="bias_ps")
         for e in range(HALVES):
@@ -126,15 +143,20 @@ def tile_list_scores_products_given_tabled_kernel(tc, xf, xb, fk, ky_words, ky_s
         bias = sb.tile([P, I], F32, name="bias")
         nc.vector.tensor_copy(out=bias[:].rearrange("p (n e) -> p n e", e=HALVES), in_=bias_ps[:].rearrange("p e n -> p n e"))
 
-        factor = [sb.tile([P, I], F32, name=f"factor_{h}") for h in range(HALVES)]
+        factor = [u32_all[1][:, 0, 2 * h : 2 * h + 2, :].rearrange("p t j -> p (t j)") for h in range(HALVES)]
         score = [sb.tile([P, I], F32, name=f"score_{h}") for h in range(HALVES)]
-        squashed = [sb.tile([P, I], F32, name=f"squashed_{h}") for h in range(HALVES)]
+        squashed_both = sb.tile([P, HALVES, I], F32, name="squashed", tag=f"tb_{HALVES - 1}")
+        squashed = [squashed_both[:, h, :] for h in range(HALVES)]
         result = [sb.tile([P, I], F32, name=f"result_{h}") for h in range(HALVES)]
         for h in range(HALVES):
-            nc.scalar.activation(factor[h][:], tb_sb[h][:].indirect(list_tb[:]), COPY)
+            nc.scalar.activation(factor[h], tb_sb[h][:].indirect(list_tb[:]), COPY)
         for h in range(HALVES):
-            nc.vector.tensor_tensor(score[h][:], acc[h][:], bias[:], ADD)
-            nc.scalar.activation(squashed[h][:], score[h][:], TANH)
+            for c in range(HALVES):
+                cols = slice(c * P, (c + 1) * P)
+                nc.vector.tensor_tensor(score[h][:, cols], acc[h, c][:], bias[:, cols], ADD)
+                nc.scalar.activation(squashed[h][:, cols], score[h][:, cols], TANH)
         for h in range(HALVES):
-            nc.vector.tensor_tensor(result[h][:], squashed[h][:], factor[h][:], MULT)
+            for c in range(HALVES):
+                cols = slice(c * P, (c + 1) * P)
+                nc.vector.tensor_tensor(result[h][:, cols], squashed[h][:, cols], factor[h][:, cols], MULT)
             nc.sync.dma_start(out=out[h * P : (h + 1) * P, :], in_=result[h][:])

@@ -39,14 +39,14 @@ def tile_list_scores_products_given_tabled_kernel(tc, xf, xb, fk, ky_words, ky_s
         list_xf = sb.tile([P, LIST_COLS], U16, name="list_xf")
         list_xb = sb.tile([P, LIST_COLS], U16, name="list_xb")
         list_tb = sb.tile([P, LIST_COLS], U16, name="list_tb")
-        fk_sb = sb.tile([P, PASSES, PACK], F32, name="fk_sb")
-        bi_cols = sb.tile([P, HALVES], F32, name="bi_cols")
+        rows = sb.tile([P, P * PACK], F32, name="rows")
         ky_codes = sb.tile([P, PASSES, I], U32, name="ky_codes", align_bytes=64)
         ky_plane = sb.tile([P, PASSES, I], U8, name="ky_plane", align_bytes=64)
         xf_sb = {(z, t0): sb.tile([P, (t1 - t0) * T], F32, name=f"xf_{z}_{t0}") for z, t0, t1 in XF_LOADS}
         xb_sb = [sb.tile([P, PACK * S], F32, name=f"xb_{z}") for z in range(PASSES)]
         tb_sb = [sb.tile([P, C], F32, name=f"tb_{h}", tag=f"tb_{h}") for h in range(HALVES)]
 
+        nc.gpsimd.memset(rows[:], 0.0)
         nc.gpsimd.memset(ky_plane[:].bitcast(I32), 0)
         ident = sb.tile([P, P], F32, name="ident")
         make_identity(nc, ident[:])
@@ -65,21 +65,36 @@ def tile_list_scores_products_given_tabled_kernel(tc, xf, xb, fk, ky_words, ky_s
             )
 
         load_xb(0)
+        nc.sync.dma_start(out=rows[0:PASSES, :], in_=fk.rearrange("(z k) o -> z (k o)", z=PASSES))
+        nc.sync.dma_start(out=rows[PASSES : PASSES + 1, 0:I], in_=bi)
         nc.sync.dma_start(list_xb[:], offs2)
         nc.sync.dma_start(list_xf[:], offs)
-        nc.sync.dma_start(out=fk_sb[:], in_=fk.rearrange("(z p t) o -> p z (t o)", p=P, t=PACK))
-        nc.sync.dma_start(out=bi_cols[:], in_=bi.rearrange("o (p h) -> p (o h)", h=HALVES))
         load_xf(0)
         nc.sync.dma_start(list_tb[:], offs3)
         load_xf(1)
+        load_scales(0)
         load_xb(1)
-        for n in range(2, len(XF_LOADS)):
+        for n in range(2, len(XF_LOADS) - 1):
+            load_scales(n - 1)
             load_xf(n)
-        for q in range(4):
-            load_scales(q)
+        load_xf(len(XF_LOADS) - 1)
         nc.sync.dma_start(out=ky_codes[:].bitcast(I32), in_=ky_words.rearrange("z p c r -> p z (c r)").bitcast(I32))
         for h in range(HALVES):
             nc.sync.dma_start(out=tb_sb[h][:], in_=tb[h * P : (h + 1) * P, :])
+
+        cols_ps = ps.tile([P, PACK, P], F32, name="cols_ps")
+        for t in range(PACK):
+            nc.tensor.transpose(cols_ps[:, t, :], rows[:, t :: PACK], ident[:])
+        cols = sb.tile([P, PACK, PASSES + 1], F32, name="cols")
+        nc.vector.tensor_copy(out=cols[:], in_=cols_ps[:, :, 0 : PASSES + 1])
+        bias_ps = ps.tile([P, PACK, P], F32, name="bias_ps")
+        for t in range(PACK):
+            nc.tensor.transpose(bias_ps[:, t, :], cols[:, t, PASSES : PASSES + 1].to_broadcast([P, P]), ident[:])
+        bias = sb.tile([P, I], F32, name="bias")
+        nc.vector.tensor_copy(
+            out=bias[:].rearrange("p (n t) -> p n t", t=PACK),
+            in_=bias_ps[:, :, 0 : I // PACK].rearrange("p t n -> p n t"),
+        )
 
         acc = {(h, c): ps.tile([P, P], F32, name=f"acc_{h}_{c}") for h in range(HALVES) for c in range(HALVES)}
         u32_all = [sb.tile([P, HALVES, PACK, P], F32, name=f"u32_{z}") for z in range(PASSES)]
@@ -101,7 +116,7 @@ def tile_list_scores_products_given_tabled_kernel(tc, xf, xb, fk, ky_words, ky_s
                         nc.vector.scalar_tensor_tensor(
                             out=u32[:, :, t, :],
                             in0=picked_xf[t - t0][:].rearrange("p (h j) -> p h j", h=HALVES),
-                            scalar=fk_sb[:, z, t : t + 1],
+                            scalar=cols[:, t, z : z + 1],
                             in1=picked_xb[t][:].rearrange("p (h j) -> p h j", h=HALVES),
                             op0=MULT,
                             op1=MULT,
@@ -110,7 +125,7 @@ def tile_list_scores_products_given_tabled_kernel(tc, xf, xb, fk, ky_words, ky_s
                 for t in range(PACK):
                     nc.scalar.activation(picked_xb[t][:], xb_sb[z][:, t * S : (t + 1) * S].indirect(list_xb[:]), COPY)
                     scaled = sb.tile([P, J], F32, name=f"scaled_{t}")
-                    nc.scalar.activation(scaled[:], picked_xb[t][:], COPY, scale=fk_sb[:, z, t : t + 1])
+                    nc.scalar.activation(scaled[:], picked_xb[t][:], COPY, scale=cols[:, t, z : z + 1])
                     for h in range(HALVES):
                         nc.vector.tensor_tensor(
                             u32[:, h, t, :],
@@ -120,8 +135,8 @@ def tile_list_scores_products_given_tabled_kernel(tc, xf, xb, fk, ky_words, ky_s
                         )
             u16 = [sb.tile([P, P, PACK], BF16, name=f"u16_{z}_{h}", tag=f"u16_{z}_{h}", align_bytes=64) for h in range(HALVES)]
             for t0, t1 in ((0, PACK),) if z == 0 else ((0, 2), (2, PACK)):
-                nc.scalar.copy(out=u16[0][:, :, t0:t1], in_=u32[:, 0, t0:t1, :].rearrange("p t j -> p j t"))
-                nc.vector.tensor_copy(out=u16[1][:, :, t0:t1], in_=u32[:, 1, t0:t1, :].rearrange("p t j -> p j t"))
+                for h in range(HALVES):
+                    nc.vector.tensor_copy(out=u16[h][:, :, t0:t1], in_=u32[:, h, t0:t1, :].rearrange("p t j -> p j t"))
             for h in range(HALVES):
                 codes = sb.tile([P, P], U32, name=f"codes_{z}_{h}", align_bytes=64)
                 plane = sb.tile([P, P], U8, name=f"plane_{z}_{h}", align_bytes=64)
@@ -137,12 +152,6 @@ def tile_list_scores_products_given_tabled_kernel(tc, xf, xb, fk, ky_words, ky_s
                         stop=(z == PASSES - 1),
                     )
 
-        bias_ps = ps.tile([P, HALVES, P], F32, name="bias_ps")
-        for e in range(HALVES):
-            nc.tensor.transpose(bias_ps[:, e, :], bi_cols[:, e : e + 1].to_broadcast([P, P]), ident[:])
-        bias = sb.tile([P, I], F32, name="bias")
-        nc.vector.tensor_copy(out=bias[:].rearrange("p (n e) -> p n e", e=HALVES), in_=bias_ps[:].rearrange("p e n -> p n e"))
-
         factor = [u32_all[1][:, 0, 2 * h : 2 * h + 2, :].rearrange("p t j -> p (t j)") for h in range(HALVES)]
         score = [sb.tile([P, I], F32, name=f"score_{h}") for h in range(HALVES)]
         squashed_both = sb.tile([P, HALVES, I], F32, name="squashed", tag=f"tb_{HALVES - 1}")
@@ -152,11 +161,11 @@ def tile_list_scores_products_given_tabled_kernel(tc, xf, xb, fk, ky_words, ky_s
             nc.scalar.activation(factor[h], tb_sb[h][:].indirect(list_tb[:]), COPY)
         for h in range(HALVES):
             for c in range(HALVES):
-                cols = slice(c * P, (c + 1) * P)
-                nc.vector.tensor_tensor(score[h][:, cols], acc[h, c][:], bias[:, cols], ADD)
-                nc.scalar.activation(squashed[h][:, cols], score[h][:, cols], TANH)
+                span = slice(c * P, (c + 1) * P)
+                nc.vector.tensor_tensor(score[h][:, span], acc[h, c][:], bias[:, span], ADD)
+                nc.scalar.activation(squashed[h][:, span], score[h][:, span], TANH)
         for h in range(HALVES):
             for c in range(HALVES):
-                cols = slice(c * P, (c + 1) * P)
-                nc.vector.tensor_tensor(result[h][:, cols], squashed[h][:, cols], factor[h][:, cols], MULT)
+                span = slice(c * P, (c + 1) * P)
+                nc.vector.tensor_tensor(result[h][:, span], squashed[h][:, span], factor[h][:, span], MULT)
             nc.sync.dma_start(out=out[h * P : (h + 1) * P, :], in_=result[h][:])

from contextlib import ExitStack

import concourse.mybir as mybir
from concourse.masks import make_identity

K, T, J, I, S, C = 1024, 1024, 256, 256, 512, 512
FLOPS = 2 * K * J * I

F32 = mybir.dt.float32
BF16 = mybir.dt.bfloat16
I32 = mybir.dt.int32
U32 = mybir.dt.uint32
U16 = mybir.dt.uint16
U8 = mybir.dt.uint8
E5M2X4 = mybir.dt.float8_e5m2_x4
MULT = mybir.AluOpType.mult
ADD = mybir.AluOpType.add
COPY = mybir.ActivationFunctionType.Copy
TANH = mybir.ActivationFunctionType.Tanh

P = 128
PACK = 4
PASSES = K // (P * PACK)
HALVES = J // P
LIST_COLS = J // 16
HALF_COLS = P // 16
XF_LOADS = ((0, 0, 2), (0, 2, 4), (1, 0, 1), (1, 1, 2), (1, 2, 3), (1, 3, 4))


def tile_list_scores_products_given_tabled_kernel(tc, xf, xb, fk, ky_words, ky_scales, bi, tb, offs, offs2, offs3, out):
    nc = tc.nc
    with ExitStack() as ctx:
        sb = ctx.enter_context(tc.tile_pool(name="sb", bufs=1))
        ps = ctx.enter_context(tc.psum_pool(name="ps", bufs=1))

        xf_rows = xf.rearrange("(z p t) n -> z p t n", p=P, t=PACK)
        xb_rows = xb.rearrange("(z p t) s -> z p t s", p=P, t=PACK)

        list_xf = sb.tile([P, LIST_COLS], U16, name="list_xf")
        list_xb = sb.tile([P, LIST_COLS], U16, name="list_xb")
        list_tb = sb.tile([P, LIST_COLS], U16, name="list_tb")
        rows = sb.tile([P, P * PACK], F32, name="rows")
        ky_codes = sb.tile([P, PASSES, I], U32, name="ky_codes", align_bytes=64)
        ky_plane = sb.tile([P, PASSES, I], U8, name="ky_plane", align_bytes=64)
        xf_sb = {(z, t0): sb.tile([P, (t1 - t0) * T], F32, name=f"xf_{z}_{t0}") for z, t0, t1 in XF_LOADS}
        xb_sb = [sb.tile([P, PACK * S], F32, name=f"xb_{z}") for z in range(PASSES)]
        tb_sb = [sb.tile([P, C], F32, name=f"tb_{h}", tag=f"tb_{h}") for h in range(HALVES)]

        nc.gpsimd.memset(rows[:], 0.0)
        nc.gpsimd.memset(ky_plane[:].bitcast(I32), 0)
        ident = sb.tile([P, P], F32, name="ident")
        make_identity(nc, ident[:])

        def load_xf(n):
            z, t0, t1 = XF_LOADS[n]
            nc.sync.dma_start(out=xf_sb[z, t0][:], in_=xf_rows[z, :, t0:t1, :].rearrange("p t n -> p (t n)"))

        def load_xb(z):
            nc.sync.dma_start(out=xb_sb[z][:], in_=xb_rows[z].rearrange("p t s -> p (t s)"))

        def load_scales(q):
            nc.sync.dma_start(
                out=ky_plane[32 * q : 32 * q + 4].bitcast(I32),
                in_=ky_scales[:, 4 * q : 4 * q + 4, :].rearrange("z r c -> r z c").bitcast(I32),
            )

        load_xb(0)
        nc.sync.dma_start(out=rows[0:PASSES, :], in_=fk.rearrange("(z k) o -> z (k o)", z=PASSES))
        nc.sync.dma_start(out=rows[PASSES : PASSES + 1, 0:I], in_=bi)
        nc.sync.dma_start(list_xb[:], offs2)
        nc.sync.dma_start(list_xf[:], offs)
        load_xf(0)
        nc.sync.dma_start(list_tb[:], offs3)
        load_xf(1)
        load_scales(0)
        load_xb(1)
        for n in range(2, len(XF_LOADS) - 1):
            load_scales(n - 1)
            load_xf(n)
        load_xf(len(XF_LOADS) - 1)
        nc.sync.dma_start(out=ky_codes[:].bitcast(I32), in_=ky_words.rearrange("z p c r -> p z (c r)").bitcast(I32))
        for h in range(HALVES):
            nc.sync.dma_start(out=tb_sb[h][:], in_=tb[h * P : (h + 1) * P, :])

        cols_ps = ps.tile([P, PACK, P], F32, name="cols_ps")
        for t in range(PACK):
            nc.tensor.transpose(cols_ps[:, t, :], rows[:, t :: PACK], ident[:])
        cols = sb.tile([P, PACK, PASSES + 1], F32, name="cols")
        nc.vector.tensor_copy(out=cols[:], in_=cols_ps[:, :, 0 : PASSES + 1])
        bias_ps = ps.tile([P, PACK, P], F32, name="bias_ps")
        for t in range(PACK):
            nc.tensor.transpose(bias_ps[:, t, :], cols[:, t, PASSES : PASSES + 1].to_broadcast([P, P]), ident[:])
        bias = sb.tile([P, I], F32, name="bias")
        nc.vector.tensor_copy(
            out=bias[:].rearrange("p (n t) -> p n t", t=PACK),
            in_=bias_ps[:, :, 0 : I // PACK].rearrange("p t n -> p n t"),
        )

        acc = {(h, c): ps.tile([P, P], F32, name=f"acc_{h}_{c}") for h in range(HALVES) for c in range(HALVES)}
        u32_all = [sb.tile([P, HALVES, PACK, P], F32, name=f"u32_{z}") for z in range(PASSES)]
        for z in range(PASSES):
            u32 = u32_all[z]
            picked_xb = [sb.tile([P, J], F32, name=f"picked_xb_{z}_{t}") for t in range(PACK)]
            if z == 0:
                for t in range(PACK):
                    window = xb_sb[z][:, t * S : (t + 1) * S].indirect(list_xb[:])
                    if t < 2:
                        nc.vector.tensor_copy(picked_xb[t][:], window)
                    else:
                        nc.scalar.activation(picked_xb[t][:], window, COPY)
                for t0 in (0, 2):
                    picked_xf = [sb.tile([P, J], F32, name=f"picked_xf_{t}") for t in (t0, t0 + 1)]
                    nc.vector.tensor_copy(picked_xf[0][:], xf_sb[z, t0][:, 0:T].indirect(list_xf[:]))
                    nc.scalar.activation(picked_xf[1][:], xf_sb[z, t0][:, T : 2 * T].indirect(list_xf[:]), COPY)
                    for t in (t0, t0 + 1):
                        nc.vector.scalar_tensor_tensor(
                            out=u32[:, :, t, :],
                            in0=picked_xf[t - t0][:].rearrange("p (h j) -> p h j", h=HALVES),
                            scalar=cols[:, t, z : z + 1],
                            in1=picked_xb[t][:].rearrange("p (h j) -> p h j", h=HALVES),
                            op0=MULT,
                            op1=MULT,
                        )
            else:
                for t in range(PACK):
                    nc.scalar.activation(picked_xb[t][:], xb_sb[z][:, t * S : (t + 1) * S].indirect(list_xb[:]), COPY)
                    scaled = sb.tile([P, J], F32, name=f"scaled_{t}")
                    nc.scalar.activation(scaled[:], picked_xb[t][:], COPY, scale=cols[:, t, z : z + 1])
                    for h in range(HALVES):
                        nc.vector.tensor_tensor(
                            u32[:, h, t, :],
                            xf_sb[z, t][:].indirect(list_xf[:, h * HALF_COLS : (h + 1) * HALF_COLS]),
                            scaled[:, h * P : (h + 1) * P],
                            MULT,
                        )
            u16 = [sb.tile([P, P, PACK], BF16, name=f"u16_{z}_{h}", tag=f"u16_{z}_{h}", align_bytes=64) for h in range(HALVES)]
            for t0, t1 in ((0, PACK),) if z == 0 else ((0, 2), (2, PACK)):
                for h in range(HALVES):
                    nc.vector.tensor_copy(out=u16[h][:, :, t0:t1], in_=u32[:, h, t0:t1, :].rearrange("p t j -> p j t"))
            for h in range(HALVES):
                codes = sb.tile([P, P], U32, name=f"codes_{z}_{h}", align_bytes=64)
                plane = sb.tile([P, P], U8, name=f"plane_{z}_{h}", align_bytes=64)
                nc.vector.quantize_mx(out=codes[:].bitcast(E5M2X4), scales=plane[:], in_=u16[h][:].rearrange("p j t -> p (j t)"))
                for c in range(HALVES):
                    nc.tensor.matmul_mx(
                        out=acc[h, c][:],
                        lhsT=codes[:].bitcast(E5M2X4),
                        lhsT_scale=plane[:],
                        rhs=ky_codes[:, z, c * P : (c + 1) * P].bitcast(E5M2X4),
                        rhs_scale=ky_plane[:, z, c * P : (c + 1) * P],
                        start=(z == 0),
                        stop=(z == PASSES - 1),
                    )

        factor = [u32_all[1][:, 0, 2 * h : 2 * h + 2, :].rearrange("p t j -> p (t j)") for h in range(HALVES)]
        score = [sb.tile([P, I], F32, name=f"score_{h}") for h in range(HALVES)]
        squashed_both = sb.tile([P, HALVES, I], F32, name="squashed", tag=f"tb_{HALVES - 1}")
        squashed = [squashed_both[:, h, :] for h in range(HALVES)]
        result = [sb.tile([P, I], F32, name=f"result_{h}") for h in range(HALVES)]
        for h in range(HALVES):
            nc.scalar.activation(factor[h], tb_sb[h][:].indirect(list_tb[:]), COPY)
        for h in range(HALVES):
            for c in range(HALVES):
                span = slice(c * P, (c + 1) * P)
                nc.vector.tensor_tensor(score[h][:, span], acc[h, c][:], bias[:, span], ADD)
                nc.scalar.activation(squashed[h][:, span], score[h][:, span], TANH)
        for h in range(HALVES):
            for c in range(HALVES):
                span = slice(c * P, (c + 1) * P)
                nc.vector.tensor_tensor(result[h][:, span], squashed[h][:, span], factor[h][:, span], MULT)
            nc.sync.dma_start(out=out[h * P : (h + 1) * P, :], in_=result[h][:])
